import numpy as np
import ml_dtypes


def mxq(x, axis, fmt="e4m3"):
    dtype, down = {"e4m3": (ml_dtypes.float8_e4m3fn, 7), "e5m2": (ml_dtypes.float8_e5m2, 14)}[fmt]
    v = np.moveaxis(np.asarray(x, np.float32).astype(ml_dtypes.bfloat16).astype(np.float64), axis, -1)
    blocks = v.reshape(v.shape[:-1] + (-1, 32))
    amax = np.abs(blocks).max(-1, keepdims=True)
    byte = np.maximum(np.where(amax > 0, np.frexp(amax)[1] - 1 + 127, 0) - down, 1)
    scale = np.exp2(byte - 127.0)
    codes = (blocks / scale).astype(np.float32).astype(dtype).astype(np.float64)
    return np.moveaxis((codes * scale).reshape(v.shape), -1, axis)


WIDE = False


def mx_kscale(k):
    if not WIDE:
        return np.ones(k)
    levels = np.array([10, -10, 5, -5, 0])
    if k % 512:
        return np.exp2(np.random.permutation(np.resize(levels, k // 32))).repeat(32)
    a = np.empty((k // 512, 16))
    for p in range(k // 512):
        a[p, :8] = np.random.permutation(np.resize(levels, 8))
        for g in range(8):
            far = levels[np.abs(levels - a[p, g]) >= 10]
            a[p, g + 8] = far[np.random.randint(len(far))]
    return np.exp2(a.ravel()).repeat(32)


def f64(x):
    return np.asarray(x).astype(np.float64)


def striped(idx):
    return np.tile(idx.reshape(-1, 16).T, (8, 1)).astype(np.uint16)


def unstriped(offs):
    return offs[:16].T.reshape(-1).astype(np.int64)


E2M1 = np.array([0.0, 0.5, 1.0, 1.5, 2.0, 3.0, 4.0, 6.0, -0.0, -0.5, -1.0, -1.5, -2.0, -3.0, -4.0, -6.0])


def pack_weight(w, fmt):
    k, n = w.shape
    w = f64(np.asarray(w, np.float32).astype(ml_dtypes.bfloat16)).reshape(k // 32, 32, n)
    amax = np.abs(w).max(1)
    if fmt == "e4m3":
        byte = np.frexp(amax)[1] - 1 + 127 - 7
    else:
        mant, ex = np.frexp(amax / 6.0)
        byte = np.where(mant > 0.5, ex, ex - 1) + 127
    byte = np.clip(np.where(amax > 0, byte, 1), 1, 254)
    scaled = (w * np.exp2(127.0 - byte)[:, None, :]).reshape(k, n).astype(np.float32)
    by_word = np.ascontiguousarray(scaled.reshape(k // 512, 128, 4, n).transpose(0, 1, 3, 2))
    if fmt == "e4m3":
        words = by_word.astype(ml_dtypes.float8_e4m3fn).view(np.uint8)
    else:
        c = by_word.astype(ml_dtypes.float4_e2m1fn).view(np.uint8) & 0xF
        words = (c[..., 0::2] | (c[..., 1::2] << 4)).reshape(k // 512, 128, 2 * n)
    return np.ascontiguousarray(words), np.ascontiguousarray(byte.astype(np.uint8).reshape(k // 512, 16, n))


def unpack_weight(words, scales, fmt):
    g, _, n = scales.shape
    words = np.ascontiguousarray(words).reshape(g, 128, n, -1)
    if fmt == "e4m3":
        vals = words.view(ml_dtypes.float8_e4m3fn).astype(np.float64)
    else:
        nib = np.empty((g, 128, n, 4), np.uint8)
        nib[..., 0::2] = words & 0xF
        nib[..., 1::2] = words >> 4
        vals = E2M1[nib]
    vals = vals * np.repeat(np.exp2(scales.astype(np.float64) - 127.0), 8, axis=1)[..., None]
    return vals.transpose(0, 1, 3, 2).reshape(g * 512, n)


def gelu(v):
    return 0.5 * v * (1.0 + np.tanh(np.sqrt(2.0 / np.pi) * (v + 0.044715 * v**3)))


def bf(x):
    return np.asarray(x, np.float32).astype(ml_dtypes.bfloat16)

def planes(Y):
    n, m = Y.shape
    b = f64(bf(Y)).reshape(n // 32, 32, m)
    amax = np.abs(b).max(1)
    byte = np.clip(np.where(amax > 0, np.frexp(amax)[1] - 1 + 127 - 7, 1), 1, 254)
    codes = (b * np.exp2(127.0 - byte)[:, None, :]).reshape(n, m).astype(np.float32).astype(ml_dtypes.float8_e4m3fn).view(np.uint8)
    words = codes.reshape(n // 512, 128, 4, m).transpose(0, 1, 3, 2)
    return np.ascontiguousarray(words), np.ascontiguousarray(byte.astype(np.uint8).reshape(n // 512, 16, m))


K, T, S, T2, S2, N = 1024, 4096, 1024, 2048, 1024, 512

def setup_inputs():
    n = np.random.standard_normal
    s = mx_kscale(K)[:, None]
    u = mx_kscale(S)[:, None]
    tab_words, tab_scales = pack_weight(np.where(n((K, T)) > 0, 1.0, -1.0) * s, "e4m3")
    tab2_words, tab2_scales = pack_weight(np.where(n((K, T2)) > 0, 1.0, -1.0) / s / np.sqrt(K), "e4m3")
    c4_words, c4_scales = pack_weight(n((S, N)) / u / np.sqrt(S), "e2m1")
    th = (2 * np.random.randint(5, 17, S) + 1) / np.sqrt(K)
    gain = np.exp(0.8 * n(N))
    return {
        "tab_words": tab_words, "tab_scales": tab_scales,
        "tab2_words": tab2_words, "tab2_scales": tab2_scales,
        "offs": striped(np.random.permutation(T)[:S]),
        "offs2": striped(np.random.permutation(T2)[:S2]),
        "th": th.astype(np.float32),
        "conf": (np.exp(0.3 * n(S)) * u[:, 0]).astype(np.float32),
        "c4_words": c4_words, "c4_scales": c4_scales,
        "wr": (0.7 * n((S, N)) / u / np.sqrt(S)).astype(np.float32),
        "gain": gain.astype(np.float32),
        "bias": (0.3 * gain * n(N)).astype(np.float32),
    }

def reference(tab_words, tab_scales, tab2_words, tab2_scales, offs, offs2, th, conf, c4_words, c4_scales, wr, gain, bias):
    v = unpack_weight(tab_words, tab_scales, "e4m3")[:, unstriped(offs)]
    v2 = unpack_weight(tab2_words, tab2_scales, "e4m3")[:, unstriped(offs2)]
    c4 = unpack_weight(c4_words, c4_scales, "e2m1")
    A = v.T @ v2
    h = np.where(A > f64(th)[:, None], 1.0, 0.0) * f64(conf)[:, None]
    hq = mxq(h, 0, "e4m3")
    r = c4.T @ hq + mxq(f64(wr), 0, "e4m3").T @ hq
    y = f64(gain)[:, None] * r + f64(bias)[:, None]
    words, scales = planes(y)
    return y, words, scales

from contextlib import ExitStack

import concourse.mybir as mybir

K, T, S, T2, S2, N = 1024, 4096, 1024, 2048, 1024, 512
FLOPS = 2 * K * S * S2 + 2 * 2 * S * N * S2

F32 = mybir.dt.float32
BF16 = mybir.dt.bfloat16
I32 = mybir.dt.int32
U32 = mybir.dt.uint32
U16 = mybir.dt.uint16
U8 = mybir.dt.uint8
FP8X4 = mybir.dt.float8_e4m3fn_x4
FP4X4 = mybir.dt.float4_e2m1fn_x4
ALU = mybir.AluOpType
ACT = mybir.ActivationFunctionType

P = 128
PACK = 4
PASS = P * PACK
J = 256
CHUNKS = S2 // J


def tile_list_kanerva_recall_kernel(
    tc, tab_words, tab_scales, tab2_words, tab2_scales, offs, offs2, th, conf,
    c4_words, c4_scales, wr, gain, bias, out_0, out_1, out_2,
):
    nc = tc.nc
    with ExitStack() as ctx:
        keep = ctx.enter_context(tc.tile_pool(name="keep", bufs=1))
        ring = ctx.enter_context(tc.tile_pool(name="ring", bufs=3))
        psum = ctx.enter_context(tc.psum_pool(name="psum", bufs=1))

        def held(name, shape, dtype, tag=None):
            return keep.tile(shape, dtype, name=name, tag=tag or name, align_bytes=64)

        offs_t = held("offs_t", [P, S // 16], U16)
        offs2_t = held("offs2_t", [P, S2 // 16], U16)
        v_tab = [held("v_tab0", [P, T], I32)]
        v2_tab = [held("v2_tab0", [P, T2], I32)]
        vs_tab = held("vs_tab", [P, T], U8)
        v2s_tab = held("v2s_tab", [P, T2], U8)
        c4s_raw = held("c4s_raw", [P, 2, N], U8)
        c4_raw = held("c4_raw", [P, 2, 2 * N], U8)
        th_t = held("th_t", [P, 2, PACK], F32)
        conf_t = held("conf_t", [P, 2, PACK], F32)

        nc.vector.memset(vs_tab[:].bitcast(I32), 0)
        nc.vector.memset(v2s_tab[:].bitcast(I32), 0)
        nc.vector.memset(c4s_raw[:].rearrange("p a n -> p (a n)").bitcast(I32), 0)

        def words(dram, a):
            return dram[a].rearrange("p n t -> p (n t)").bitcast(I32)

        nc.sync.dma_start(offs2_t[:], offs2)
        nc.sync.dma_start(offs_t[:], offs)
        nc.sync.dma_start(out=th_t[:], in_=th.rearrange("(b p t) -> p b t", b=2, t=PACK))
        nc.sync.dma_start(out=conf_t[:], in_=conf.rearrange("(b p t) -> p b t", b=2, t=PACK))
        nc.sync.dma_start(out=v2_tab[0][:], in_=words(tab2_words, 0))
        nc.sync.dma_start(out=v_tab[0][:], in_=words(tab_words, 0))
        nc.sync.dma_start(out=c4_raw[:].bitcast(I32), in_=c4_words.rearrange("a p n -> p a n").bitcast(I32))
        for q in range(4):
            nc.gpsimd.dma_start(
                out=vs_tab[32 * q : 32 * q + 8, :].bitcast(I32),
                in_=tab_scales[:, 4 * q : 4 * q + 4, :].bitcast(I32),
            )
        for q in range(4):
            nc.scalar.dma_start(
                out=v2s_tab[32 * q + 8 : 32 * q + 16, :].bitcast(I32),
                in_=tab2_scales[:, 4 * q : 4 * q + 4, :].bitcast(I32),
            )
        for q in range(4):
            nc.scalar.dma_start(
                out=c4s_raw[32 * q : 32 * q + 4, :, :].bitcast(I32),
                in_=c4_scales[:, 4 * q : 4 * q + 4, :].rearrange("a r n -> r a n").bitcast(I32),
            )

        v2_first = held("v2_first", [P, S2], U32)
        nc.vector.tensor_copy(v2_first[:], v2_tab[0][:].bitcast(U32).indirect(offs2_t[:]))
        v_tab.append(held("v_tab1", [P, T], I32, tag="v2_tab0"))
        nc.sync.dma_start(out=v_tab[1][:], in_=words(tab_words, 1))
        v2s = held("v2s", [P, S2], U8)
        nc.vector.tensor_copy(v2s[:], v2s_tab[:].indirect(offs2_t[:]))
        v2_tab.append(held("v2_tab1", [P, T2], I32, tag="v2s_tab"))
        nc.sync.dma_start(out=v2_tab[1][:], in_=words(tab2_words, 1))
        vs_listed = held("vs_listed", [P, S], U8)
        nc.vector.tensor_copy(vs_listed[:], vs_tab[:].indirect(offs_t[:]))
        vs = held("vs", [P, S], U8)
        nc.vector.tensor_copy(
            out=vs[:].rearrange("q (b t p) -> q b t p", b=2, t=PACK),
            in_=vs_listed[:].rearrange("q (b p t) -> q b t p", b=2, t=PACK),
        )
        v = [
            [held("v00", [P, PASS], U32, tag="vs_tab"), held("v01", [P, PASS], U32, tag="vs_listed")],
            [held("v10", [P, PASS], U32), held("v11", [P, PASS], U32)],
        ]

        def gather_v(a, b):
            nc.vector.tensor_copy(
                v[a][b][:].rearrange("q (t p) -> q p t", t=PACK),
                v_tab[a][:].bitcast(U32).indirect(offs_t[:, 32 * b : 32 * (b + 1)]),
            )

        v2_second = [held(f"v2_second{c}", [P, J], U32) for c in range(CHUNKS)]

        def gather_v2(c):
            nc.vector.tensor_copy(
                v2_second[c][:],
                v2_tab[1][:].bitcast(U32).indirect(offs2_t[:, (J // 16) * c : (J // 16) * (c + 1)]),
            )

        def bank(k):
            return psum.tile([P, 2, J], F32, name=f"bank{k}")

        def a_pass(banks, c, a, b, u):
            cols = slice(J * c, J * (c + 1))
            rhs = v2_first[:, cols] if a == 0 else v2_second[c][:]
            for e in range(2):
                t = 2 * u + e
                nc.tensor.matmul_mx(
                    out=banks[2 * b + u][:, e, :],
                    lhsT=v[a][b][:, P * t : P * (t + 1)].bitcast(FP8X4),
                    lhsT_scale=vs[4 * a : P, PASS * b + P * t : PASS * b + P * (t + 1)],
                    rhs=rhs.bitcast(FP8X4),
                    rhs_scale=v2s[8 + 4 * a : P, cols],
                    start=(a == 0 and e == 0),
                    stop=(a == 1 and e == 1),
                )

        def signs(banks, b):
            sg = ring.tile([P, PACK, J], BF16, name="sg", align_bytes=64)
            for t in range(PACK):
                nc.scalar.activation(
                    out=sg[:, t, :], in_=banks[2 * b + t // 2][:, t % 2, :], func=ACT.Sign,
                    bias=th_t[:, b, t : t + 1], scale=-1.0,
                )
            return sg

        hq = [[held(f"hq{c}{b}", [P, J], U32) for b in range(2)] for c in range(CHUNKS)]
        hs = [[held(f"hs{c}{b}", [P, J], U8) for b in range(2)] for c in range(CHUNKS)]

        def weigh(sg, b):
            hp = ring.tile([P, PACK, J], BF16, name="hp", align_bytes=64)
            for t in range(PACK):
                nc.vector.tensor_scalar(
                    out=hp[:, t, :], in0=sg[:, t, :], scalar1=0.0, scalar2=conf_t[:, b, t : t + 1],
                    op0=ALU.is_lt, op1=ALU.mult,
                )
            return hp

        def weave(planes):
            woven = ring.tile([P, J * PACK], BF16, name="woven", align_bytes=64)
            nc.vector.tensor_copy(
                out=woven[:].rearrange("p (c i t) -> p c t i", i=4, t=PACK),
                in_=planes[:].rearrange("p t (c i) -> p c t i", i=4),
            )
            return woven

        def h_stage(banks, c, b):
            woven = weave(weigh(signs(banks, b), b))
            nc.vector.quantize_mx(out=hq[c][b][:].bitcast(FP8X4), scales=hs[c][b][:], in_=woven[:])

        c4 = held("c4", [P, 2, 2 * N], U8)
        c4s = held("c4s", [P, 2, N], U8)
        wr_bf = [held(f"wr_bf{b}", [P, PACK * N], BF16) for b in range(2)]
        wq = [held(f"wq{b}", [P, N], U32) for b in range(2)]
        ws = [held(f"ws{b}", [P, N], U8) for b in range(2)]

        def wr_round(b, copy):
            copy(
                out=wr_bf[b][:].rearrange("p (s m t) -> p m s t", s=PACK, t=PACK),
                in_=wr_raw[:, b].rearrange("p t (m s) -> p m s t", s=PACK),
            )

        def wr_quantize(b):
            nc.vector.quantize_mx(out=wq[b][:].bitcast(FP8X4), scales=ws[b][:], in_=wr_bf[b][:])

        def r_stage(banks, c):
            order = [(w, b) for b in range(2) for w in range(2)]
            for n, (w, b) in enumerate(order):
                for s in range(PACK):
                    if w == 0:
                        lhsT = c4[:, b, 2 * P * s : 2 * P * (s + 1)].bitcast(FP4X4)
                        lhsT_scale = c4s[:, b, P * s : P * (s + 1)]
                    else:
                        lhsT = wq[b][:, P * s : P * (s + 1)].bitcast(FP8X4)
                        lhsT_scale = ws[b][:, P * s : P * (s + 1)]
                    nc.tensor.matmul_mx(
                        out=banks[s // 2][:, s % 2, :], lhsT=lhsT, lhsT_scale=lhsT_scale,
                        rhs=hq[c][b][:].bitcast(FP8X4), rhs_scale=hs[c][b][:],
                        start=(n == 0 and s % 2 == 0), stop=(n == 3 and s % 2 == 1),
                    )

        yq = [held(f"yq{c}", [P, J], U32) for c in range(CHUNKS)]
        ys = held("ys", [P, S2], U8)
        out_rows = out_0.rearrange("(p s) j -> p s j", s=PACK)
        out_words = words(out_1, 0)

        def y_stage(banks, c):
            cols = slice(J * c, J * (c + 1))
            y = held(f"y{c}", [P, PACK, J], F32)
            for s in range(PACK):
                nc.scalar.activation(
                    out=y[:, s, :], in_=banks[s // 2][:, s % 2, :], func=ACT.Identity,
                    bias=bias_t[:, s : s + 1], scale=gain_t[:, s : s + 1],
                )
            nc.sync.dma_start(out=out_rows[:, :, cols], in_=y[:])
            woven = weave(y)
            nc.vector.quantize_mx(out=yq[c][:].bitcast(FP8X4), scales=ys[:, cols], in_=woven[:])
            nc.sync.dma_start(out=out_words[:, cols], in_=yq[c][:].bitcast(I32))

        nc.scalar.copy(
            out=c4[:].bitcast(U16).rearrange("p a (s m) -> p a m s", s=PACK),
            in_=c4_raw[:].bitcast(U16).rearrange("p a (m s) -> p a m s", s=PACK),
        )
        gain_t = held("gain_t", [P, PACK], F32, tag="c4_raw")
        nc.scalar.dma_start(out=gain_t[:], in_=gain.rearrange("(p t) -> p t", t=PACK))
        for b in range(2):
            gather_v(0, b)
        wr_raw = held("wr_raw", [P, 2, PACK, N], F32, tag="v_tab0")
        for b in range(2):
            nc.sync.dma_start(
                out=wr_raw[:, b], in_=wr[PASS * b : PASS * (b + 1), :].rearrange("(p t) n -> p t n", t=PACK)
            )
        a_banks = [[bank(k) for k in range(4)], [bank(k) for k in range(4, 8)]]
        for c in range(2):
            for b in range(2):
                for u in range(2):
                    a_pass(a_banks[c], c, 0, b, u)
        nc.vector.tensor_copy(
            out=c4s[:].rearrange("p a (s m) -> p a s m", s=PACK),
            in_=c4s_raw[:].rearrange("p a (m s) -> p a s m", s=PACK),
        )
        bias_t = held("bias_t", [P, PACK], F32, tag="c4s_raw")
        nc.scalar.dma_start(out=bias_t[:], in_=bias.rearrange("(p t) -> p t", t=PACK))
        for b in range(2):
            gather_v(1, b)
        gather_v2(0)
        gather_v2(1)
        for c in range(2):
            for b in range(2):
                for u in range(2):
                    a_pass(a_banks[c], c, 1, b, u)

        def a_stage(banks, c):
            for b in range(2):
                for u in range(2):
                    for a in range(2):
                        a_pass(banks, c, a, b, u)

        gather_v2(2)
        h_stage(a_banks[0], 0, 0)
        gather_v2(3)
        h_stage(a_banks[0], 0, 1)
        a2 = [bank(k) for k in range(4)]
        a_stage(a2, 2)
        wr_round(0, nc.vector.tensor_copy)
        h_stage(a_banks[1], 1, 0)
        wr_quantize(0)
        h_stage(a_banks[1], 1, 1)
        wr_round(1, nc.scalar.copy)
        wr_quantize(1)
        r0 = [bank(4), bank(5)]
        r_stage(r0, 0)
        h_stage(a2, 2, 0)
        h_stage(a2, 2, 1)
        a3 = [bank(k) for k in range(4)]
        a_stage(a3, 3)
        r1 = [bank(6), bank(7)]
        r_stage(r1, 1)
        y_stage(r0, 0)
        h_stage(a3, 3, 0)
        h_stage(a3, 3, 1)
        r2 = [bank(4), bank(5)]
        r_stage(r2, 2)
        y_stage(r1, 1)
        r3 = [bank(6), bank(7)]
        r_stage(r3, 3)
        y_stage(r2, 2)
        y_stage(r3, 3)
        for q in range(4):
            queue = nc.scalar if q % 2 else nc.sync
            queue.dma_start(
                out=out_2[0, 4 * q : 4 * q + 4, :].bitcast(I32), in_=ys[32 * q : 32 * q + 4, :].bitcast(I32)
            )
